import numpy as np
import ml_dtypes


def mxq(x, axis, fmt="e4m3"):
    dtype, down = {"e4m3": (ml_dtypes.float8_e4m3fn, 7), "e5m2": (ml_dtypes.float8_e5m2, 14)}[fmt]
    v = np.moveaxis(np.asarray(x, np.float32).astype(ml_dtypes.bfloat16).astype(np.float64), axis, -1)
    blocks = v.reshape(v.shape[:-1] + (-1, 32))
    amax = np.abs(blocks).max(-1, keepdims=True)
    byte = np.maximum(np.where(amax > 0, np.frexp(amax)[1] - 1 + 127, 0) - down, 1)
    scale = np.exp2(byte - 127.0)
    codes = (blocks / scale).astype(np.float32).astype(dtype).astype(np.float64)
    return np.moveaxis((codes * scale).reshape(v.shape), -1, axis)


WIDE = False


def mx_kscale(k):
    if not WIDE:
        return np.ones(k)
    levels = np.array([10, -10, 5, -5, 0])
    if k % 512:
        return np.exp2(np.random.permutation(np.resize(levels, k // 32))).repeat(32)
    a = np.empty((k // 512, 16))
    for p in range(k // 512):
        a[p, :8] = np.random.permutation(np.resize(levels, 8))
        for g in range(8):
            far = levels[np.abs(levels - a[p, g]) >= 10]
            a[p, g + 8] = far[np.random.randint(len(far))]
    return np.exp2(a.ravel()).repeat(32)


def f64(x):
    return np.asarray(x).astype(np.float64)


def striped(idx):
    return np.tile(idx.reshape(-1, 16).T, (8, 1)).astype(np.uint16)


def unstriped(offs):
    return offs[:16].T.reshape(-1).astype(np.int64)


def striped8(idx):
    return np.concatenate([x.reshape(-1, 16).T for x in idx]).astype(np.uint16)


def runs(offs, k):
    lists = np.stack([offs[16 * r : 16 * r + 16].T.reshape(-1) for r in range(8)]).astype(np.int64)
    return lists[np.arange(k) % 512 // 64]


def pack_weight(w):
    k, n = w.shape
    w = f64(np.asarray(w, np.float32).astype(ml_dtypes.bfloat16)).reshape(k // 32, 32, n)
    amax = np.abs(w).max(1)
    byte = np.clip(np.where(amax > 0, np.frexp(amax)[1] - 1 + 127 - 7, 1), 1, 254)
    scaled = (w * np.exp2(127.0 - byte)[:, None, :]).reshape(k, n).astype(np.float32)
    words = np.ascontiguousarray(scaled.reshape(k // 512, 128, 4, n).transpose(0, 1, 3, 2)).astype(ml_dtypes.float8_e4m3fn).view(np.uint8)
    return words, np.ascontiguousarray(byte.astype(np.uint8).reshape(k // 512, 16, n))


def unpack_weight(words, scales):
    g, p, n, _ = words.shape
    vals = np.ascontiguousarray(words).view(ml_dtypes.float8_e4m3fn).astype(np.float64) * np.repeat(np.exp2(scales.astype(np.float64) - 127.0), 8, axis=1)[..., None]
    return vals.transpose(0, 1, 3, 2).reshape(g * 512, n)

def planes(y):
    n, m = y.shape
    v = y.astype(np.float32).astype(ml_dtypes.bfloat16).astype(np.float64).reshape(n // 32, 32, m)
    top = np.abs(v).max(1)
    byte = np.clip(np.where(top > 0, np.frexp(top)[1] - 1 + 127 - 7, 1), 1, 254)
    codes = (v * np.exp2(127.0 - byte)[:, None, :]).reshape(n, m).astype(np.float32).astype(ml_dtypes.float8_e4m3fn).view(np.uint8)
    words = codes.reshape(n // 512, 128, 4, m).transpose(0, 1, 3, 2)
    return np.ascontiguousarray(words), np.ascontiguousarray(byte.astype(np.uint8).reshape(n // 512, 16, m))


K, T, S, V, N, H = 512, 2048, 1024, 512, 512, 512


def setup_inputs():
    n = np.random.standard_normal
    s = mx_kscale(K)[:, None]
    u = mx_kscale(H)
    packed_xT = pack_weight(n((K, T)) * s)
    packed_w3 = pack_weight(n((H, N)) / np.sqrt(H) / u[:, None])
    return {
        "x_words": packed_xT[0],
        "x_scales": packed_xT[1],
        "w1": (n((K, H)) / np.sqrt(K) / s * u).astype(np.float32),
        "w2": (n((H, H)) / np.sqrt(H) / u[:, None] * u).astype(np.float32),
        "w3_words": packed_w3[0],
        "w3_scales": packed_w3[1],
        "res": n((N, V)).astype(np.float32),
        "offs": striped(np.random.permutation(T)[:S]),
        "n1": striped8(np.stack([np.random.permutation(S) for _ in range(8)])),
        "n2": striped8(np.stack([np.random.permutation(V) for _ in range(8)])),
    }


def reference(x_words, x_scales, w1, w2, w3_words, w3_scales, res, offs, n1, n2):
    xq = unpack_weight(x_words, x_scales)[:, unstriped(offs)]
    y = mxq(f64(w1), 0, "e4m3").T @ xq
    ln = y[np.arange(H)[:, None], runs(n1, H)]
    z = ln.reshape(H, V, 2).max(axis=2)
    h = mxq(f64(w2), 0, "e4m3").T @ mxq(z, 0, "e4m3")
    z2 = np.maximum(h, h[np.arange(H)[:, None], runs(n2, H)])
    out_0 = f64(res) + (unpack_weight(w3_words, w3_scales).T @ mxq(z2, 0, "e4m3"))
    return (out_0,) + planes(out_0)

@@ -1,0 +1,223 @@
+from contextlib import ExitStack
+
+import concourse.mybir as mybir
+
+K, T, S, V, N, H = 512, 2048, 1024, 512, 512, 512
+FLOPS = 2 * K * H * S + 2 * H * H * V + 2 * H * N * V
+
+F32 = mybir.dt.float32
+BF16 = mybir.dt.bfloat16
+I32 = mybir.dt.int32
+U32 = mybir.dt.uint32
+U16 = mybir.dt.uint16
+U8 = mybir.dt.uint8
+FP8X4 = mybir.dt.float8_e4m3fn_x4
+MAX = mybir.AluOpType.max
+ADD = mybir.AluOpType.add
+
+P = 128
+PACK = 4
+BANK = 512
+PIECE = 128
+Z_PIECES = [(0, 256), (256, 128), (384, 128)]
+G2_PIECES = [(0, 256), (256, 256)]
+
+
+def tile_picked_deeppoolbig_none_po_kernel(
+    tc, x_words, x_scales, w1, w2, w3_words, w3_scales, res, offs, n1, n2, out_0, out_1, out_2
+):
+    nc = tc.nc
+
+    def words_i32(ap):
+        return ap[0].rearrange("p n t -> p (n t)").bitcast(I32)
+
+    def mx(out, w_codes, w_scales, a_codes, a_scales):
+        nc.tensor.matmul_mx(
+            out=out, lhsT=w_codes.bitcast(FP8X4), lhsT_scale=w_scales,
+            rhs=a_codes.bitcast(FP8X4), rhs_scale=a_scales, start=True, stop=True,
+        )
+
+    def quantize(codes, scales, values):
+        nc.vector.quantize_mx(out=codes.bitcast(FP8X4), scales=scales, in_=values)
+
+    with ExitStack() as ctx:
+        lists = ctx.enter_context(tc.tile_pool(name="lists", bufs=1))
+        sb = ctx.enter_context(tc.tile_pool(name="sb", bufs=1))
+        psum = ctx.enter_context(tc.psum_pool(name="psum", bufs=8))
+
+        def tile(shape, dtype, name, tag=None):
+            return sb.tile(shape, dtype, name=name, tag=tag or name, align_bytes=64)
+
+        offs_t = lists.tile([P, S // 16], U16, name="offs_t")
+        n1_t = lists.tile([P, S // 16], U16, name="n1_t")
+        n2_t = lists.tile([P, V // 16], U16, name="n2_t")
+
+        xs_all = tile([P, T], U8, "xs_all", "scale_rows")
+        nc.vector.memset(xs_all[:].bitcast(I32), 0)
+        nc.sync.dma_start(offs_t[:], offs)
+        xw_all = tile([P, T], U32, "xw_all", "packed")
+        nc.sync.dma_start(out=xw_all[:].bitcast(I32), in_=words_i32(x_words))
+        for q in range(4):
+            nc.sync.dma_start(
+                out=xs_all[:].bitcast(I32)[32 * q : 32 * q + 4, :], in_=x_scales[0].bitcast(I32)[4 * q : 4 * q + 4, :]
+            )
+        w1_raw = tile([P, PACK, H], F32, "w1_raw", "raw")
+        nc.sync.dma_start(out=w1_raw[:], in_=w1.rearrange("(p j) c -> p j c", j=PACK))
+        nc.sync.dma_start(n1_t[:], n1)
+        nc.sync.dma_start(n2_t[:], n2)
+
+        xw = [tile([P, BANK], U32, f"xw{half}") for half in range(2)]
+        xs = [tile([P, BANK], U8, "xs0")]
+        nc.vector.tensor_copy(xw[0][:], xw_all[:].indirect(offs_t[:, 0:32]))
+        nc.vector.tensor_copy(xs[0][:], xs_all[:].indirect(offs_t[:, 0:32]))
+        nc.vector.tensor_copy(xw[1][:], xw_all[:].indirect(offs_t[:, 32:64]))
+
+        w1_view = w1_raw[:].rearrange("p j (b t h i) -> p t b h j i", t=PACK, h=2, i=4)
+        w1_codes, w1_scales = [], []
+        for t in range(PACK):
+            grouped = tile([P, P * PACK], BF16, f"w1_bf{t}")
+            dst = grouped[:].rearrange("p (b h i j) -> p b h j i", h=2, i=4, j=PACK)
+            nc.scalar.copy(dst, w1_view[:, t])
+            codes = tile([P, P], U32, f"w1_codes{t}")
+            scales = tile([P, P], U8, f"w1_scales{t}")
+            quantize(codes[:], scales[:], grouped[:])
+            w1_codes.append(codes)
+            w1_scales.append(scales)
+            if t == 1:
+                xs.append(tile([P, BANK], U8, "xs1", "w1_bf0"))
+                nc.vector.tensor_copy(xs[1][:], xs_all[:].indirect(offs_t[:, 32:64]))
+
+        w3w_raw = tile([P, N], U32, "w3w_raw", "packed")
+        nc.sync.dma_start(out=w3w_raw[:].bitcast(I32), in_=words_i32(w3_words))
+        w3s_raw = tile([P, N], U8, "w3s_raw", "scale_rows")
+        nc.vector.memset(w3s_raw[:].bitcast(I32), 0)
+        for q in range(4):
+            nc.sync.dma_start(
+                out=w3s_raw[:].bitcast(I32)[32 * q : 32 * q + 4, :], in_=w3_scales[0].bitcast(I32)[4 * q : 4 * q + 4, :]
+            )
+        w2_raw = tile([P, PACK, H], F32, "w2_raw", "raw")
+        w2_rows = w2.rearrange("(b j i) c -> j b i c", j=PACK, i=8)
+        for j in range(PACK):
+            nc.sync.dma_start(out=w2_raw[:, j, :], in_=w2_rows[j])
+
+        y = []
+        for t in range(PACK):
+            y_t = tile([P, S], F32, f"y{t}")
+            for half in range(2):
+                parts = 2 if t == 0 and half == 1 else 1
+                width = BANK // parts
+                for part in range(parts):
+                    cols = slice(part * width, (part + 1) * width)
+                    acc = psum.tile([P, width], F32, name="bank")
+                    mx(acc[:], w1_codes[t][:], w1_scales[t][:], xw[half][:, cols], xs[half][:, cols])
+                    dst = y_t[:, half * BANK + part * width : half * BANK + (part + 1) * width]
+                    if parts == 2 and part == 1:
+                        nc.vector.tensor_copy(dst, acc[:])
+                    else:
+                        nc.scalar.copy(dst, acc[:])
+            y.append(y_t)
+
+        w2_bf = tile([P, H * PACK], BF16, "w2_bf")
+        w2_dst = w2_bf[:].rearrange("p (t m j) -> p m j t", t=PACK, j=PACK)
+        w2_src = w2_raw[:].rearrange("p j (m t) -> p m j t", t=PACK)
+        for half in range(2):
+            nc.scalar.copy(w2_dst[:, 64 * half : 64 * half + 64], w2_src[:, 64 * half : 64 * half + 64])
+        res_t = tile([P, PACK, V], F32, "res_t", "xw0")
+        nc.sync.dma_start(out=res_t[:], in_=res.rearrange("(p t) v -> p t v", t=PACK))
+        w2_codes = tile([P, H], U32, "w2_codes")
+        w2_scales = tile([P, H], U8, "w2_scales")
+
+        h = [tile([P, V], F32, f"h{t}") for t in range(PACK)]
+        h_acc = []
+        h_bf = []
+        for v0, n in Z_PIECES:
+            last = v0 + n == V
+            lined = tile([P, PACK, 2 * n], F32, f"lined{v0}", "raw" if last else None)
+            for t in range(PACK):
+                nc.vector.tensor_copy(lined[:, t, :], y[t][:].indirect(n1_t[:, v0 // 8 : (v0 + n) // 8]))
+            if v0 == 0:
+                quantize(w2_codes[:], w2_scales[:], w2_bf[:])
+            for c0 in range(0, n, PIECE):
+                c = (v0 + c0) // PIECE
+                piece = lined[:, :, 2 * c0 : 2 * (c0 + PIECE)]
+                z_bf = tile([P, PACK * PIECE], BF16, f"z_bf{c}")
+                if last or not False:
+                    pairs = piece.rearrange("p t (c i e) -> p e c t i", i=2, e=2)
+                    nc.vector.tensor_tensor(
+                        z_bf[:].rearrange("p (c i t) -> p c t i", i=2, t=PACK), pairs[:, 0], pairs[:, 1], MAX
+                    )
+                else:
+                    sides = tile([P, 2, PACK * PIECE], BF16, f"sides{c}")
+                    nc.scalar.copy(
+                        sides[:].rearrange("p e (c i t) -> p c t i e", i=2, t=PACK),
+                        piece.rearrange("p t (c i e) -> p c t i e", i=2, e=2),
+                    )
+                    nc.vector.tensor_tensor(z_bf[:], sides[:, 0, :], sides[:, 1, :], MAX)
+                z_codes = tile([P, PIECE], U32, f"z_codes{c}")
+                z_scales = tile([P, PIECE], U8, f"z_scales{c}")
+                quantize(z_codes[:], z_scales[:], z_bf[:])
+                acc = psum.tile([P, PACK, PIECE], F32, name="bank")
+                cols = slice(c * PIECE, (c + 1) * PIECE)
+                for t in range(PACK):
+                    rows = slice(t * P, (t + 1) * P)
+                    mx(acc[:, t, :], w2_codes[:, rows], w2_scales[:, rows], z_codes[:], z_scales[:])
+                    if last:
+                        nc.scalar.copy(h[t][:, cols], acc[:, t, :])
+                if not last:
+                    for t in range(PACK):
+                        nc.scalar.copy(h[t][:, cols], acc[:, t, :])
+                h_acc.append(acc)
+
+        w3_codes = tile([P, N], U32, "w3_codes", "z_bf3")
+        nc.vector.tensor_copy(
+            w3_codes[:].rearrange("p (t c i) -> p c t i", t=PACK, i=4),
+            w3w_raw[:].rearrange("p (c i t) -> p c t i", t=PACK, i=4),
+        )
+        w3_sc = tile([P, N], U8, "w3_sc", "z_bf2")
+        nc.vector.tensor_copy(
+            w3_sc[:].rearrange("p (t m) -> p t m", t=PACK),
+            w3s_raw[:].rearrange("p (m t) -> p t m", t=PACK),
+        )
+
+        out_rows = out_0.rearrange("(p t) v -> p t v", t=PACK)
+        out_words = words_i32(out_1)
+        o_scales = tile([P, V], U8, "o_scales")
+        for v0, n in G2_PIECES:
+            partner = tile([P, PACK, n], F32, f"partner{v0}")
+            for t in range(PACK):
+                nc.vector.tensor_copy(partner[:, t, :], h[t][:].indirect(n2_t[:, v0 // 16 : (v0 + n) // 16]))
+            for c0 in range(0, n, PIECE):
+                c = (v0 + c0) // PIECE
+                cols = slice(v0 + c0, v0 + c0 + PIECE)
+                z2_bf = tile([P, PACK * PIECE], BF16, f"z2_bf{c}")
+                nc.vector.tensor_tensor(
+                    z2_bf[:].rearrange("p (c i t) -> p c t i", i=4, t=PACK),
+                    partner[:, :, c0 : c0 + PIECE].rearrange("p t (c i) -> p c t i", i=4),
+                    h_acc[c][:].rearrange("p t (c i) -> p c t i", i=4),
+                    MAX,
+                )
+                z2_codes = tile([P, PIECE], U32, f"z2_codes{c}")
+                z2_scales = tile([P, PIECE], U8, f"z2_scales{c}")
+                quantize(z2_codes[:], z2_scales[:], z2_bf[:])
+                acc = psum.tile([P, PACK, PIECE], F32, name="bank")
+                for t in range(PACK):
+                    rows = slice(t * P, (t + 1) * P)
+                    mx(acc[:, t, :], w3_codes[:, rows], w3_sc[:, rows], z2_codes[:], z2_scales[:])
+                o = tile([P, PACK, PIECE], F32, f"o{c}")
+                nc.vector.tensor_tensor(o[:], acc[:], res_t[:, :, cols], ADD)
+                nc.sync.dma_start(out=out_rows[:, :, cols], in_=o[:])
+                o_bf = tile([P, PACK * PIECE], BF16, f"o_bf{c}")
+                dst = o_bf[:].rearrange("p (c i t) -> p c t i", i=4, t=PACK)
+                src = o[:].rearrange("p t (c i) -> p c t i", i=4)
+                if c == V // PIECE - 1:
+                    nc.vector.tensor_copy(dst, src)
+                else:
+                    nc.scalar.copy(dst, src)
+                o_codes = tile([P, PIECE], U32, f"o_codes{c}")
+                quantize(o_codes[:], o_scales[:, cols], o_bf[:])
+                nc.sync.dma_start(out=out_words[:, cols], in_=o_codes[:].bitcast(I32))
+        for q in range(4):
+            queue = nc.scalar if q % 2 == 0 else nc.sync
+            queue.dma_start(
+                out=out_2[0].bitcast(I32)[4 * q : 4 * q + 4, :], in_=o_scales[:].bitcast(I32)[32 * q : 32 * q + 4, :]
+            )

@@ -19,6 +19,7 @@ P = 128
 PACK = 4
 BANK = 512
 PIECE = 128
+X_FIRST = 512
 Z_PIECES = [(0, 256), (256, 128), (384, 128)]
 G2_PIECES = [(0, 256), (256, 256)]
 
@@ -56,20 +57,22 @@ def tile_picked_deeppoolbig_none_po_kernel(
         nc.vector.memset(xs_all[:].bitcast(I32), 0)
         nc.sync.dma_start(offs_t[:], offs)
         xw_all = tile([P, T], U32, "xw_all", "packed")
-        nc.sync.dma_start(out=xw_all[:].bitcast(I32), in_=words_i32(x_words))
+        nc.sync.dma_start(out=xw_all[:, :X_FIRST].bitcast(I32), in_=words_i32(x_words)[:, :X_FIRST])
         for q in range(4):
             nc.sync.dma_start(
                 out=xs_all[:].bitcast(I32)[32 * q : 32 * q + 4, :], in_=x_scales[0].bitcast(I32)[4 * q : 4 * q + 4, :]
             )
+        nc.sync.dma_start(out=xw_all[:, X_FIRST:].bitcast(I32), in_=words_i32(x_words)[:, X_FIRST:])
         w1_raw = tile([P, PACK, H], F32, "w1_raw", "raw")
         nc.sync.dma_start(out=w1_raw[:], in_=w1.rearrange("(p j) c -> p j c", j=PACK))
         nc.sync.dma_start(n1_t[:], n1)
         nc.sync.dma_start(n2_t[:], n2)
 
         xw = [tile([P, BANK], U32, f"xw{half}") for half in range(2)]
-        xs = [tile([P, BANK], U8, "xs0")]
+        xs_t = tile([P, S], U8, "xs_t")
+        nc.vector.tensor_copy(xs_t[:], xs_all[:].indirect(offs_t[:]))
+        xs = [xs_t[:, :BANK], xs_t[:, BANK:]]
         nc.vector.tensor_copy(xw[0][:], xw_all[:].indirect(offs_t[:, 0:32]))
-        nc.vector.tensor_copy(xs[0][:], xs_all[:].indirect(offs_t[:, 0:32]))
         nc.vector.tensor_copy(xw[1][:], xw_all[:].indirect(offs_t[:, 32:64]))
 
         w1_view = w1_raw[:].rearrange("p j (b t h i) -> p t b h j i", t=PACK, h=2, i=4)
@@ -83,11 +86,13 @@ def tile_picked_deeppoolbig_none_po_kernel(
             quantize(codes[:], scales[:], grouped[:])
             w1_codes.append(codes)
             w1_scales.append(scales)
-            if t == 1:
-                xs.append(tile([P, BANK], U8, "xs1", "w1_bf0"))
-                nc.vector.tensor_copy(xs[1][:], xs_all[:].indirect(offs_t[:, 32:64]))
 
-        w3w_raw = tile([P, N], U32, "w3w_raw", "packed")
+        w2_raw = tile([P, PACK, H], F32, "w2_raw", "packed")
+        w2_rows = w2.rearrange("(b j i) c -> j b i c", j=PACK, i=8)
+        for j in range(PACK):
+            nc.sync.dma_start(out=w2_raw[:, j, :], in_=w2_rows[j])
+
+        w3w_raw = tile([P, N], U32, "w3w_raw", "raw")
         nc.sync.dma_start(out=w3w_raw[:].bitcast(I32), in_=words_i32(w3_words))
         w3s_raw = tile([P, N], U8, "w3s_raw", "scale_rows")
         nc.vector.memset(w3s_raw[:].bitcast(I32), 0)
@@ -95,127 +100,128 @@ def tile_picked_deeppoolbig_none_po_kernel(
             nc.sync.dma_start(
                 out=w3s_raw[:].bitcast(I32)[32 * q : 32 * q + 4, :], in_=w3_scales[0].bitcast(I32)[4 * q : 4 * q + 4, :]
             )
-        w2_raw = tile([P, PACK, H], F32, "w2_raw", "raw")
-        w2_rows = w2.rearrange("(b j i) c -> j b i c", j=PACK, i=8)
-        for j in range(PACK):
-            nc.sync.dma_start(out=w2_raw[:, j, :], in_=w2_rows[j])
-
         y = []
         for t in range(PACK):
             y_t = tile([P, S], F32, f"y{t}")
             for half in range(2):
-                parts = 2 if t == 0 and half == 1 else 1
+                parts = 2 if t == 0 else 1
                 width = BANK // parts
                 for part in range(parts):
                     cols = slice(part * width, (part + 1) * width)
                     acc = psum.tile([P, width], F32, name="bank")
                     mx(acc[:], w1_codes[t][:], w1_scales[t][:], xw[half][:, cols], xs[half][:, cols])
                     dst = y_t[:, half * BANK + part * width : half * BANK + (part + 1) * width]
-                    if parts == 2 and part == 1:
+                    if parts == 2 and (half, part) != (1, 1):
                         nc.vector.tensor_copy(dst, acc[:])
                     else:
                         nc.scalar.copy(dst, acc[:])
             y.append(y_t)
 
-        w2_bf = tile([P, H * PACK], BF16, "w2_bf")
+        w2_bf = tile([P, H * PACK], BF16, "w2_bf", "xw1")
         w2_dst = w2_bf[:].rearrange("p (t m j) -> p m j t", t=PACK, j=PACK)
         w2_src = w2_raw[:].rearrange("p j (m t) -> p m j t", t=PACK)
-        for half in range(2):
-            nc.scalar.copy(w2_dst[:, 64 * half : 64 * half + 64], w2_src[:, 64 * half : 64 * half + 64])
+        for part in range(2):
+            nc.scalar.copy(w2_dst[:, 64 * part : 64 * part + 64], w2_src[:, 64 * part : 64 * part + 64])
         res_t = tile([P, PACK, V], F32, "res_t", "xw0")
         nc.sync.dma_start(out=res_t[:], in_=res.rearrange("(p t) v -> p t v", t=PACK))
         w2_codes = tile([P, H], U32, "w2_codes")
         w2_scales = tile([P, H], U8, "w2_scales")
 
         h = [tile([P, V], F32, f"h{t}") for t in range(PACK)]
-        h_acc = []
-        h_bf = []
-        for v0, n in Z_PIECES:
-            last = v0 + n == V
-            lined = tile([P, PACK, 2 * n], F32, f"lined{v0}", "raw" if last else None)
+
+        def line_up(v0, n, tag=None):
+            lined = tile([P, PACK, 2 * n], BF16, f"lined{v0}", tag)
             for t in range(PACK):
                 nc.vector.tensor_copy(lined[:, t, :], y[t][:].indirect(n1_t[:, v0 // 8 : (v0 + n) // 8]))
-            if v0 == 0:
-                quantize(w2_codes[:], w2_scales[:], w2_bf[:])
-            for c0 in range(0, n, PIECE):
-                c = (v0 + c0) // PIECE
-                piece = lined[:, :, 2 * c0 : 2 * (c0 + PIECE)]
-                z_bf = tile([P, PACK * PIECE], BF16, f"z_bf{c}")
-                if last or not False:
-                    pairs = piece.rearrange("p t (c i e) -> p e c t i", i=2, e=2)
-                    nc.vector.tensor_tensor(
-                        z_bf[:].rearrange("p (c i t) -> p c t i", i=2, t=PACK), pairs[:, 0], pairs[:, 1], MAX
-                    )
-                else:
-                    sides = tile([P, 2, PACK * PIECE], BF16, f"sides{c}")
-                    nc.scalar.copy(
-                        sides[:].rearrange("p e (c i t) -> p c t i e", i=2, t=PACK),
-                        piece.rearrange("p t (c i e) -> p c t i e", i=2, e=2),
-                    )
-                    nc.vector.tensor_tensor(z_bf[:], sides[:, 0, :], sides[:, 1, :], MAX)
-                z_codes = tile([P, PIECE], U32, f"z_codes{c}")
-                z_scales = tile([P, PIECE], U8, f"z_scales{c}")
-                quantize(z_codes[:], z_scales[:], z_bf[:])
-                acc = psum.tile([P, PACK, PIECE], F32, name="bank")
-                cols = slice(c * PIECE, (c + 1) * PIECE)
+            return lined
+
+        lined_a = line_up(0, 256)
+        lined_b = line_up(256, 128)
+        lined = {0: lined_a[:, :, 0:256], 1: lined_a[:, :, 256:512], 2: lined_b[:]}
+        quantize(w2_codes[:], w2_scales[:], w2_bf[:])
+
+        h_acc = {}
+        for c in range(4):
+            z_bf = tile([P, PACK * PIECE], BF16, f"z_bf{c}")
+            pairs = lined[c].rearrange("p t (c i e) -> p e c t i", i=4, e=2)
+            nc.vector.tensor_tensor(
+                z_bf[:].rearrange("p (c i t) -> p c t i", i=4, t=PACK), pairs[:, 0], pairs[:, 1], MAX
+            )
+            z_codes = tile([P, PIECE], U32, f"z_codes{c}")
+            z_scales = tile([P, PIECE], U8, f"z_scales{c}")
+            quantize(z_codes[:], z_scales[:], z_bf[:])
+            if c == 2:
+                lined[3] = line_up(384, 128, "z_bf0")[:]
+            acc = psum.tile([P, PACK, PIECE], F32, name="bank")
+            cols = slice(c * PIECE, (c + 1) * PIECE)
+            for t in range(PACK):
+                rows = slice(t * P, (t + 1) * P)
+                mx(acc[:, t, :], w2_codes[:, rows], w2_scales[:, rows], z_codes[:], z_scales[:])
+                if c == 3 and True:
+                    nc.scalar.copy(h[t][:, cols], acc[:, t, :])
+            if c != 3 or not True:
                 for t in range(PACK):
-                    rows = slice(t * P, (t + 1) * P)
-                    mx(acc[:, t, :], w2_codes[:, rows], w2_scales[:, rows], z_codes[:], z_scales[:])
-                    if last:
-                        nc.scalar.copy(h[t][:, cols], acc[:, t, :])
-                if not last:
-                    for t in range(PACK):
-                        nc.scalar.copy(h[t][:, cols], acc[:, t, :])
-                h_acc.append(acc)
+                    nc.scalar.copy(h[t][:, cols], acc[:, t, :])
+            h_acc[c] = acc
 
         w3_codes = tile([P, N], U32, "w3_codes", "z_bf3")
         nc.vector.tensor_copy(
             w3_codes[:].rearrange("p (t c i) -> p c t i", t=PACK, i=4),
             w3w_raw[:].rearrange("p (c i t) -> p c t i", t=PACK, i=4),
         )
-        w3_sc = tile([P, N], U8, "w3_sc", "z_bf2")
+        w3_sc = tile([P, N], U8, "w3_sc", "z_bf0")
         nc.vector.tensor_copy(
             w3_sc[:].rearrange("p (t m) -> p t m", t=PACK),
             w3s_raw[:].rearrange("p (m t) -> p t m", t=PACK),
         )
 
+        partner = {}
+        for v0, n in [(128, 128), (256, 256), (0, 128)]:
+            fetched = tile([P, PACK, n], F32, f"partner{v0}")
+            for t in range(PACK):
+                nc.vector.tensor_copy(fetched[:, t, :], h[t][:].indirect(n2_t[:, v0 // 16 : (v0 + n) // 16]))
+            for c0 in range(0, n, PIECE):
+                partner[(v0 + c0) // PIECE] = fetched[:, :, c0 : c0 + PIECE].rearrange("p t (c i) -> p c t i", i=4)
+        h_bf, partner_bf = {}, {}
+        for c in (1, 2, 3):
+            h_bf[c] = tile([P, PACK * PIECE], BF16, f"h_bf{c}")
+            nc.scalar.copy(h_bf[c][:].rearrange("p (v t) -> p v t", t=PACK), h_acc[c][:].rearrange("p t v -> p v t"))
+            partner_bf[c] = tile([P, PACK * PIECE], BF16, f"partner_bf{c}")
+            nc.scalar.copy(partner_bf[c][:].rearrange("p (c i t) -> p c t i", i=4, t=PACK), partner[c])
+
         out_rows = out_0.rearrange("(p t) v -> p t v", t=PACK)
         out_words = words_i32(out_1)
         o_scales = tile([P, V], U8, "o_scales")
-        for v0, n in G2_PIECES:
-            partner = tile([P, PACK, n], F32, f"partner{v0}")
-            for t in range(PACK):
-                nc.vector.tensor_copy(partner[:, t, :], h[t][:].indirect(n2_t[:, v0 // 16 : (v0 + n) // 16]))
-            for c0 in range(0, n, PIECE):
-                c = (v0 + c0) // PIECE
-                cols = slice(v0 + c0, v0 + c0 + PIECE)
-                z2_bf = tile([P, PACK * PIECE], BF16, f"z2_bf{c}")
+        for c in range(V // PIECE):
+            cols = slice(c * PIECE, (c + 1) * PIECE)
+            z2_bf = tile([P, PACK * PIECE], BF16, f"z2_bf{c}")
+            if c == 0:
                 nc.vector.tensor_tensor(
                     z2_bf[:].rearrange("p (c i t) -> p c t i", i=4, t=PACK),
-                    partner[:, :, c0 : c0 + PIECE].rearrange("p t (c i) -> p c t i", i=4),
-                    h_acc[c][:].rearrange("p t (c i) -> p c t i", i=4),
-                    MAX,
+                    partner[c], h_acc[c][:].rearrange("p t (c i) -> p c t i", i=4), MAX,
                 )
-                z2_codes = tile([P, PIECE], U32, f"z2_codes{c}")
-                z2_scales = tile([P, PIECE], U8, f"z2_scales{c}")
-                quantize(z2_codes[:], z2_scales[:], z2_bf[:])
-                acc = psum.tile([P, PACK, PIECE], F32, name="bank")
-                for t in range(PACK):
-                    rows = slice(t * P, (t + 1) * P)
-                    mx(acc[:, t, :], w3_codes[:, rows], w3_sc[:, rows], z2_codes[:], z2_scales[:])
-                o = tile([P, PACK, PIECE], F32, f"o{c}")
-                nc.vector.tensor_tensor(o[:], acc[:], res_t[:, :, cols], ADD)
-                nc.sync.dma_start(out=out_rows[:, :, cols], in_=o[:])
-                o_bf = tile([P, PACK * PIECE], BF16, f"o_bf{c}")
-                dst = o_bf[:].rearrange("p (c i t) -> p c t i", i=4, t=PACK)
-                src = o[:].rearrange("p t (c i) -> p c t i", i=4)
-                if c == V // PIECE - 1:
-                    nc.vector.tensor_copy(dst, src)
-                else:
-                    nc.scalar.copy(dst, src)
-                o_codes = tile([P, PIECE], U32, f"o_codes{c}")
-                quantize(o_codes[:], o_scales[:, cols], o_bf[:])
-                nc.sync.dma_start(out=out_words[:, cols], in_=o_codes[:].bitcast(I32))
+            else:
+                nc.vector.tensor_tensor(z2_bf[:], partner_bf[c][:], h_bf[c][:], MAX)
+            z2_codes = tile([P, PIECE], U32, f"z2_codes{c}")
+            z2_scales = tile([P, PIECE], U8, f"z2_scales{c}")
+            quantize(z2_codes[:], z2_scales[:], z2_bf[:])
+            acc = psum.tile([P, PACK, PIECE], F32, name="bank")
+            for t in range(PACK):
+                rows = slice(t * P, (t + 1) * P)
+                mx(acc[:, t, :], w3_codes[:, rows], w3_sc[:, rows], z2_codes[:], z2_scales[:])
+            o = tile([P, PACK, PIECE], F32, f"o{c}")
+            nc.vector.tensor_tensor(o[:], acc[:], res_t[:, :, cols], ADD)
+            nc.sync.dma_start(out=out_rows[:, :, cols], in_=o[:])
+            o_bf = tile([P, PACK * PIECE], BF16, f"o_bf{c}")
+            dst = o_bf[:].rearrange("p (c i t) -> p c t i", i=4, t=PACK)
+            src = o[:].rearrange("p t (c i) -> p c t i", i=4)
+            if c == V // PIECE - 1:
+                nc.vector.tensor_copy(dst, src)
+            else:
+                nc.scalar.copy(dst, src)
+            o_codes = tile([P, PIECE], U32, f"o_codes{c}")
+            quantize(o_codes[:], o_scales[:, cols], o_bf[:])
+            nc.sync.dma_start(out=out_words[:, cols], in_=o_codes[:].bitcast(I32))
         for q in range(4):
             queue = nc.scalar if q % 2 == 0 else nc.sync
             queue.dma_start(

@@ -17,11 +17,12 @@ ADD = mybir.AluOpType.add
 
 P = 128
 PACK = 4
+QUADRANTS = 4
 BANK = 512
 PIECE = 128
-X_FIRST = 512
-Z_PIECES = [(0, 256), (256, 128), (384, 128)]
-G2_PIECES = [(0, 256), (256, 256)]
+PIECES = V // PIECE
+LIST_ROWS = 16
+X_FIRST = 256
 
 
 def tile_picked_deeppoolbig_none_po_kernel(
@@ -29,201 +30,206 @@ def tile_picked_deeppoolbig_none_po_kernel(
 ):
     nc = tc.nc
 
-    def words_i32(ap):
-        return ap[0].rearrange("p n t -> p (n t)").bitcast(I32)
+    def words_i32(packed):
+        return packed[0].rearrange("p n t -> p (n t)").bitcast(I32)
 
-    def mx(out, w_codes, w_scales, a_codes, a_scales):
+    def scale_rows(plane, rows, q):
+        return plane[:].bitcast(I32)[32 * q : 32 * q + 4, :], rows[0].bitcast(I32)[4 * q : 4 * q + 4, :]
+
+    def entries(list_tile, first, count):
+        return list_tile[:, first // LIST_ROWS : (first + count) // LIST_ROWS]
+
+    def product(out, w_codes, w_scales, a_codes, a_scales):
         nc.tensor.matmul_mx(
-            out=out, lhsT=w_codes.bitcast(FP8X4), lhsT_scale=w_scales,
-            rhs=a_codes.bitcast(FP8X4), rhs_scale=a_scales, start=True, stop=True,
+            out=out,
+            lhsT=w_codes.bitcast(FP8X4),
+            lhsT_scale=w_scales,
+            rhs=a_codes.bitcast(FP8X4),
+            rhs_scale=a_scales,
+            start=True,
+            stop=True,
         )
-
-    def quantize(codes, scales, values):
-        nc.vector.quantize_mx(out=codes.bitcast(FP8X4), scales=scales, in_=values)
 
     with ExitStack() as ctx:
         lists = ctx.enter_context(tc.tile_pool(name="lists", bufs=1))
-        sb = ctx.enter_context(tc.tile_pool(name="sb", bufs=1))
+        sbuf = ctx.enter_context(tc.tile_pool(name="sbuf", bufs=1))
         psum = ctx.enter_context(tc.psum_pool(name="psum", bufs=8))
 
-        def tile(shape, dtype, name, tag=None):
-            return sb.tile(shape, dtype, name=name, tag=tag or name, align_bytes=64)
+        def tile(shape, dtype, name, after=None):
+            return sbuf.tile(shape, dtype, name=name, tag=after or name, align_bytes=64)
 
-        offs_t = lists.tile([P, S // 16], U16, name="offs_t")
-        n1_t = lists.tile([P, S // 16], U16, name="n1_t")
-        n2_t = lists.tile([P, V // 16], U16, name="n2_t")
+        def quantize(values, name):
+            width = values.shape[1] // PACK
+            codes = tile([P, width], U32, f"{name}_codes")
+            scales = tile([P, width], U8, f"{name}_scales")
+            nc.vector.quantize_mx(out=codes[:].bitcast(FP8X4), scales=scales[:], in_=values)
+            return codes, scales
 
-        xs_all = tile([P, T], U8, "xs_all", "scale_rows")
+        def woven(flat):
+            return flat.rearrange("p (c i t) -> p c t i", i=4, t=PACK)
+
+        def planes(stacked):
+            return stacked.rearrange("p t (c i) -> p c t i", i=4)
+
+        offs_t = lists.tile([P, S // LIST_ROWS], U16, name="offs_t")
+        n1_t = lists.tile([P, S // LIST_ROWS], U16, name="n1_t")
+        n2_t = lists.tile([P, V // LIST_ROWS], U16, name="n2_t")
+        xs_all = tile([P, T], U8, "xs_all")
+        xw_all = tile([P, T], U32, "xw_all")
+        w1_raw = tile([P, PACK, H], F32, "w1_raw")
         nc.vector.memset(xs_all[:].bitcast(I32), 0)
         nc.sync.dma_start(offs_t[:], offs)
-        xw_all = tile([P, T], U32, "xw_all", "packed")
         nc.sync.dma_start(out=xw_all[:, :X_FIRST].bitcast(I32), in_=words_i32(x_words)[:, :X_FIRST])
-        for q in range(4):
-            nc.sync.dma_start(
-                out=xs_all[:].bitcast(I32)[32 * q : 32 * q + 4, :], in_=x_scales[0].bitcast(I32)[4 * q : 4 * q + 4, :]
-            )
+        for q in range(QUADRANTS):
+            in_sbuf, in_hbm = scale_rows(xs_all, x_scales, q)
+            nc.sync.dma_start(out=in_sbuf, in_=in_hbm)
         nc.sync.dma_start(out=xw_all[:, X_FIRST:].bitcast(I32), in_=words_i32(x_words)[:, X_FIRST:])
-        w1_raw = tile([P, PACK, H], F32, "w1_raw", "raw")
         nc.sync.dma_start(out=w1_raw[:], in_=w1.rearrange("(p j) c -> p j c", j=PACK))
         nc.sync.dma_start(n1_t[:], n1)
         nc.sync.dma_start(n2_t[:], n2)
 
-        xw = [tile([P, BANK], U32, f"xw{half}") for half in range(2)]
-        xs_t = tile([P, S], U8, "xs_t")
-        nc.vector.tensor_copy(xs_t[:], xs_all[:].indirect(offs_t[:]))
-        xs = [xs_t[:, :BANK], xs_t[:, BANK:]]
-        nc.vector.tensor_copy(xw[0][:], xw_all[:].indirect(offs_t[:, 0:32]))
-        nc.vector.tensor_copy(xw[1][:], xw_all[:].indirect(offs_t[:, 32:64]))
+        xs = tile([P, S], U8, "xs")
+        nc.vector.tensor_copy(xs[:], xs_all[:].indirect(offs_t[:]))
+        xw = [tile([P, BANK], U32, f"xw{half}") for half in range(S // BANK)]
+        for half in range(S // BANK):
+            nc.vector.tensor_copy(xw[half][:], xw_all[:].indirect(entries(offs_t, half * BANK, BANK)))
 
         w1_view = w1_raw[:].rearrange("p j (b t h i) -> p t b h j i", t=PACK, h=2, i=4)
-        w1_codes, w1_scales = [], []
+        w1_mx = []
         for t in range(PACK):
-            grouped = tile([P, P * PACK], BF16, f"w1_bf{t}")
-            dst = grouped[:].rearrange("p (b h i j) -> p b h j i", h=2, i=4, j=PACK)
-            nc.scalar.copy(dst, w1_view[:, t])
-            codes = tile([P, P], U32, f"w1_codes{t}")
-            scales = tile([P, P], U8, f"w1_scales{t}")
-            quantize(codes[:], scales[:], grouped[:])
-            w1_codes.append(codes)
-            w1_scales.append(scales)
+            w1_bf = tile([P, P * PACK], BF16, f"w1_bf{t}")
+            nc.scalar.copy(w1_bf[:].rearrange("p (b h i j) -> p b h j i", h=2, i=4, j=PACK), w1_view[:, t])
+            w1_mx.append(quantize(w1_bf[:], f"w1_{t}"))
 
-        w2_raw = tile([P, PACK, H], F32, "w2_raw", "packed")
+        w2_raw = tile([P, PACK, H], F32, "w2_raw", after="xw_all")
         w2_rows = w2.rearrange("(b j i) c -> j b i c", j=PACK, i=8)
         for j in range(PACK):
             nc.sync.dma_start(out=w2_raw[:, j, :], in_=w2_rows[j])
-
-        w3w_raw = tile([P, N], U32, "w3w_raw", "raw")
+        w3w_raw = tile([P, N], U32, "w3w_raw", after="w1_raw")
         nc.sync.dma_start(out=w3w_raw[:].bitcast(I32), in_=words_i32(w3_words))
-        w3s_raw = tile([P, N], U8, "w3s_raw", "scale_rows")
+        w3s_raw = tile([P, N], U8, "w3s_raw", after="xs_all")
         nc.vector.memset(w3s_raw[:].bitcast(I32), 0)
-        for q in range(4):
-            nc.sync.dma_start(
-                out=w3s_raw[:].bitcast(I32)[32 * q : 32 * q + 4, :], in_=w3_scales[0].bitcast(I32)[4 * q : 4 * q + 4, :]
-            )
+        for q in range(QUADRANTS):
+            in_sbuf, in_hbm = scale_rows(w3s_raw, w3_scales, q)
+            nc.sync.dma_start(out=in_sbuf, in_=in_hbm)
+
         y = []
         for t in range(PACK):
             y_t = tile([P, S], F32, f"y{t}")
-            for half in range(2):
-                parts = 2 if t == 0 else 1
-                width = BANK // parts
-                for part in range(parts):
-                    cols = slice(part * width, (part + 1) * width)
-                    acc = psum.tile([P, width], F32, name="bank")
-                    mx(acc[:], w1_codes[t][:], w1_scales[t][:], xw[half][:, cols], xs[half][:, cols])
-                    dst = y_t[:, half * BANK + part * width : half * BANK + (part + 1) * width]
-                    if parts == 2 and (half, part) != (1, 1):
-                        nc.vector.tensor_copy(dst, acc[:])
-                    else:
-                        nc.scalar.copy(dst, acc[:])
+            codes, scales = w1_mx[t]
+            width = BANK // 2 if t == 0 else BANK
+            for first in range(0, S, width):
+                cols = slice(first, first + width)
+                acc = psum.tile([P, width], F32, name="bank")
+                product(acc[:], codes[:], scales[:], xw[first // BANK][:, first % BANK : first % BANK + width], xs[:, cols])
+                if t == 0 and first + width < S:
+                    nc.vector.tensor_copy(y_t[:, cols], acc[:])
+                else:
+                    nc.scalar.copy(y_t[:, cols], acc[:])
             y.append(y_t)
 
-        w2_bf = tile([P, H * PACK], BF16, "w2_bf", "xw1")
+        w2_bf = tile([P, H * PACK], BF16, "w2_bf", after="xw1")
         w2_dst = w2_bf[:].rearrange("p (t m j) -> p m j t", t=PACK, j=PACK)
         w2_src = w2_raw[:].rearrange("p j (m t) -> p m j t", t=PACK)
-        for part in range(2):
-            nc.scalar.copy(w2_dst[:, 64 * part : 64 * part + 64], w2_src[:, 64 * part : 64 * part + 64])
-        res_t = tile([P, PACK, V], F32, "res_t", "xw0")
+        for half in range(2):
+            nc.scalar.copy(w2_dst[:, 64 * half : 64 * half + 64], w2_src[:, 64 * half : 64 * half + 64])
+        res_t = tile([P, PACK, V], F32, "res_t", after="xw0")
         nc.sync.dma_start(out=res_t[:], in_=res.rearrange("(p t) v -> p t v", t=PACK))
-        w2_codes = tile([P, H], U32, "w2_codes")
-        w2_scales = tile([P, H], U8, "w2_scales")
 
-        h = [tile([P, V], F32, f"h{t}") for t in range(PACK)]
-
-        def line_up(v0, n, tag=None):
-            lined = tile([P, PACK, 2 * n], BF16, f"lined{v0}", tag)
+        def line_up(first, count, dtype, after=None):
+            lined = tile([P, PACK, 2 * count], dtype, f"lined{first}", after)
             for t in range(PACK):
-                nc.vector.tensor_copy(lined[:, t, :], y[t][:].indirect(n1_t[:, v0 // 8 : (v0 + n) // 8]))
+                nc.vector.tensor_copy(lined[:, t, :], y[t][:].indirect(entries(n1_t, 2 * first, 2 * count)))
             return lined
 
-        lined_a = line_up(0, 256)
-        lined_b = line_up(256, 128)
-        lined = {0: lined_a[:, :, 0:256], 1: lined_a[:, :, 256:512], 2: lined_b[:]}
-        quantize(w2_codes[:], w2_scales[:], w2_bf[:])
-
-        h_acc = {}
-        for c in range(4):
-            z_bf = tile([P, PACK * PIECE], BF16, f"z_bf{c}")
-            pairs = lined[c].rearrange("p t (c i e) -> p e c t i", i=4, e=2)
-            nc.vector.tensor_tensor(
-                z_bf[:].rearrange("p (c i t) -> p c t i", i=4, t=PACK), pairs[:, 0], pairs[:, 1], MAX
+        lined_a = line_up(0, PIECE, F32)
+        lined_b = line_up(PIECE, 2 * PIECE, F32)
+        sides = []
+        for c, lined in enumerate([lined_a[:], lined_b[:, :, : 2 * PIECE], lined_b[:, :, 2 * PIECE :]]):
+            both = tile([P, 2, PACK * PIECE], BF16, f"sides{c}")
+            nc.scalar.copy(
+                both[:].rearrange("p e (c i t) -> p c t i e", i=2, t=PACK),
+                lined.rearrange("p t (c i e) -> p c t i e", i=2, e=2),
             )
-            z_codes = tile([P, PIECE], U32, f"z_codes{c}")
-            z_scales = tile([P, PIECE], U8, f"z_scales{c}")
-            quantize(z_codes[:], z_scales[:], z_bf[:])
-            if c == 2:
-                lined[3] = line_up(384, 128, "z_bf0")[:]
-            acc = psum.tile([P, PACK, PIECE], F32, name="bank")
-            cols = slice(c * PIECE, (c + 1) * PIECE)
+            sides.append(both)
+        w2_codes, w2_scales = quantize(w2_bf[:], "w2")
+
+        h = [tile([P, V], F32, f"h{t}") for t in range(PACK)]
+        h_acc = [psum.tile([P, V], F32, name="bank") for t in range(PACK)]
+
+        def hidden(z_bf, first):
+            z_codes, z_scales = quantize(z_bf[:], f"z{first}")
+            cols = slice(first, first + z_codes.shape[1])
             for t in range(PACK):
                 rows = slice(t * P, (t + 1) * P)
-                mx(acc[:, t, :], w2_codes[:, rows], w2_scales[:, rows], z_codes[:], z_scales[:])
-                if c == 3 and True:
-                    nc.scalar.copy(h[t][:, cols], acc[:, t, :])
-            if c != 3 or not True:
-                for t in range(PACK):
-                    nc.scalar.copy(h[t][:, cols], acc[:, t, :])
-            h_acc[c] = acc
+                product(h_acc[t][:, cols], w2_codes[:, rows], w2_scales[:, rows], z_codes[:], z_scales[:])
+                nc.scalar.copy(h[t][:, cols], h_acc[t][:, cols])
 
-        w3_codes = tile([P, N], U32, "w3_codes", "z_bf3")
+        for c in range(2):
+            z_bf = tile([P, PACK * PIECE], BF16, f"z_bf{c}")
+            nc.vector.tensor_tensor(z_bf[:], sides[c][:, 0, :], sides[c][:, 1, :], MAX)
+            hidden(z_bf, c * PIECE)
+        lined_c = line_up(3 * PIECE, PIECE, BF16, after="sides0")
+        z_rest = tile([P, 2 * PACK * PIECE], BF16, "z_rest")
+        nc.vector.tensor_tensor(z_rest[:, : PACK * PIECE], sides[2][:, 0, :], sides[2][:, 1, :], MAX)
+        pairs = lined_c[:].rearrange("p t (c i e) -> p e c t i", i=4, e=2)
+        nc.vector.tensor_tensor(woven(z_rest[:, PACK * PIECE :]), pairs[:, 0], pairs[:, 1], MAX)
+        hidden(z_rest, 2 * PIECE)
+
+        w3_codes = tile([P, N], U32, "w3_codes", after="z_rest")
         nc.vector.tensor_copy(
             w3_codes[:].rearrange("p (t c i) -> p c t i", t=PACK, i=4),
             w3w_raw[:].rearrange("p (c i t) -> p c t i", t=PACK, i=4),
         )
-        w3_sc = tile([P, N], U8, "w3_sc", "z_bf0")
+        w3_bytes = tile([P, N], U8, "w3_bytes", after="sides0")
         nc.vector.tensor_copy(
-            w3_sc[:].rearrange("p (t m) -> p t m", t=PACK),
-            w3s_raw[:].rearrange("p (m t) -> p t m", t=PACK),
+            w3_bytes[:].rearrange("p (t m) -> p t m", t=PACK), w3s_raw[:].rearrange("p (m t) -> p t m", t=PACK)
         )
 
-        partner = {}
-        for v0, n in [(128, 128), (256, 256), (0, 128)]:
-            fetched = tile([P, PACK, n], F32, f"partner{v0}")
+        h_bf = tile([P, PACK, V], BF16, "h_bf")
+        for t in range(PACK):
+            nc.scalar.copy(h_bf[:, t, :], h_acc[t][:])
+        z2_bf = [tile([P, PACK * PIECE], BF16, f"z2_bf{c}") for c in range(PIECES)]
+
+        def fetch_partners(first, count, after=None):
+            partner = tile([P, PACK, count], BF16, f"partner{first}", after)
             for t in range(PACK):
-                nc.vector.tensor_copy(fetched[:, t, :], h[t][:].indirect(n2_t[:, v0 // 16 : (v0 + n) // 16]))
-            for c0 in range(0, n, PIECE):
-                partner[(v0 + c0) // PIECE] = fetched[:, :, c0 : c0 + PIECE].rearrange("p t (c i) -> p c t i", i=4)
-        h_bf, partner_bf = {}, {}
-        for c in (1, 2, 3):
-            h_bf[c] = tile([P, PACK * PIECE], BF16, f"h_bf{c}")
-            nc.scalar.copy(h_bf[c][:].rearrange("p (v t) -> p v t", t=PACK), h_acc[c][:].rearrange("p t v -> p v t"))
-            partner_bf[c] = tile([P, PACK * PIECE], BF16, f"partner_bf{c}")
-            nc.scalar.copy(partner_bf[c][:].rearrange("p (c i t) -> p c t i", i=4, t=PACK), partner[c])
+                nc.vector.tensor_copy(partner[:, t, :], h[t][:].indirect(entries(n2_t, first, count)))
+            return partner[:], h_bf[:, :, first : first + count]
+
+        for first, count in ((0, PIECE), (PIECE, 2 * PIECE)):
+            partner, own = fetch_partners(first, count)
+            larger = tile([P, PACK, count], BF16, f"larger{first}")
+            nc.vector.tensor_tensor(larger[:], partner, own, MAX)
+            for offset in range(0, count, PIECE):
+                nc.scalar.copy(woven(z2_bf[(first + offset) // PIECE][:]), planes(larger[:, :, offset : offset + PIECE]))
 
         out_rows = out_0.rearrange("(p t) v -> p t v", t=PACK)
-        out_words = words_i32(out_1)
-        o_scales = tile([P, V], U8, "o_scales")
-        for c in range(V // PIECE):
+        out_scales = tile([P, V], U8, "out_scales")
+
+        def finish(c, round_on):
             cols = slice(c * PIECE, (c + 1) * PIECE)
-            z2_bf = tile([P, PACK * PIECE], BF16, f"z2_bf{c}")
-            if c == 0:
-                nc.vector.tensor_tensor(
-                    z2_bf[:].rearrange("p (c i t) -> p c t i", i=4, t=PACK),
-                    partner[c], h_acc[c][:].rearrange("p t (c i) -> p c t i", i=4), MAX,
-                )
-            else:
-                nc.vector.tensor_tensor(z2_bf[:], partner_bf[c][:], h_bf[c][:], MAX)
-            z2_codes = tile([P, PIECE], U32, f"z2_codes{c}")
-            z2_scales = tile([P, PIECE], U8, f"z2_scales{c}")
-            quantize(z2_codes[:], z2_scales[:], z2_bf[:])
+            z2_codes, z2_scales = quantize(z2_bf[c][:], f"z2_{c}")
             acc = psum.tile([P, PACK, PIECE], F32, name="bank")
             for t in range(PACK):
                 rows = slice(t * P, (t + 1) * P)
-                mx(acc[:, t, :], w3_codes[:, rows], w3_sc[:, rows], z2_codes[:], z2_scales[:])
-            o = tile([P, PACK, PIECE], F32, f"o{c}")
-            nc.vector.tensor_tensor(o[:], acc[:], res_t[:, :, cols], ADD)
-            nc.sync.dma_start(out=out_rows[:, :, cols], in_=o[:])
-            o_bf = tile([P, PACK * PIECE], BF16, f"o_bf{c}")
-            dst = o_bf[:].rearrange("p (c i t) -> p c t i", i=4, t=PACK)
-            src = o[:].rearrange("p t (c i) -> p c t i", i=4)
-            if c == V // PIECE - 1:
-                nc.vector.tensor_copy(dst, src)
-            else:
-                nc.scalar.copy(dst, src)
-            o_codes = tile([P, PIECE], U32, f"o_codes{c}")
-            quantize(o_codes[:], o_scales[:, cols], o_bf[:])
-            nc.sync.dma_start(out=out_words[:, cols], in_=o_codes[:].bitcast(I32))
-        for q in range(4):
+                product(acc[:, t, :], w3_codes[:, rows], w3_bytes[:, rows], z2_codes[:], z2_scales[:])
+            total = tile([P, PACK, PIECE], F32, f"total{c}")
+            nc.vector.tensor_tensor(total[:], acc[:], res_t[:, :, cols], ADD)
+            nc.sync.dma_start(out=out_rows[:, :, cols], in_=total[:])
+            total_bf = tile([P, PACK * PIECE], BF16, f"total_bf{c}")
+            round_on(woven(total_bf[:]), planes(total[:]))
+            out_codes = tile([P, PIECE], U32, f"out_codes{c}")
+            nc.vector.quantize_mx(out=out_codes[:].bitcast(FP8X4), scales=out_scales[:, cols], in_=total_bf[:])
+            nc.sync.dma_start(out=words_i32(out_1)[:, cols], in_=out_codes[:].bitcast(I32))
+
+        finish(0, nc.scalar.copy)
+        partner, own = fetch_partners(3 * PIECE, PIECE, after="partner0")
+        nc.vector.tensor_tensor(woven(z2_bf[3][:]), planes(partner), planes(own), MAX)
+        finish(1, nc.scalar.copy)
+        finish(3, nc.scalar.copy)
+        finish(2, nc.vector.tensor_copy)
+        for q in range(QUADRANTS):
+            in_sbuf, in_hbm = scale_rows(out_scales, out_2, q)
             queue = nc.scalar if q % 2 == 0 else nc.sync
-            queue.dma_start(
-                out=out_2[0].bitcast(I32)[4 * q : 4 * q + 4, :], in_=o_scales[:].bitcast(I32)[32 * q : 32 * q + 4, :]
-            )
+            queue.dma_start(out=in_hbm, in_=in_sbuf)

from contextlib import ExitStack

import concourse.mybir as mybir

K, T, S, V, N, H = 512, 2048, 1024, 512, 512, 512
FLOPS = 2 * K * H * S + 2 * H * H * V + 2 * H * N * V

F32 = mybir.dt.float32
BF16 = mybir.dt.bfloat16
I32 = mybir.dt.int32
U32 = mybir.dt.uint32
U16 = mybir.dt.uint16
U8 = mybir.dt.uint8
FP8X4 = mybir.dt.float8_e4m3fn_x4
MAX = mybir.AluOpType.max
ADD = mybir.AluOpType.add

P = 128
PACK = 4
QUADRANTS = 4
BANK = 512
PIECE = 128
PIECES = V // PIECE
LIST_ROWS = 16
X_FIRST = 256


def tile_picked_deeppoolbig_none_po_kernel(
    tc, x_words, x_scales, w1, w2, w3_words, w3_scales, res, offs, n1, n2, out_0, out_1, out_2
):
    nc = tc.nc

    def words_i32(packed):
        return packed[0].rearrange("p n t -> p (n t)").bitcast(I32)

    def scale_rows(plane, rows, q):
        return plane[:].bitcast(I32)[32 * q : 32 * q + 4, :], rows[0].bitcast(I32)[4 * q : 4 * q + 4, :]

    def entries(list_tile, first, count):
        return list_tile[:, first // LIST_ROWS : (first + count) // LIST_ROWS]

    def product(out, w_codes, w_scales, a_codes, a_scales):
        nc.tensor.matmul_mx(
            out=out,
            lhsT=w_codes.bitcast(FP8X4),
            lhsT_scale=w_scales,
            rhs=a_codes.bitcast(FP8X4),
            rhs_scale=a_scales,
            start=True,
            stop=True,
        )

    with ExitStack() as ctx:
        lists = ctx.enter_context(tc.tile_pool(name="lists", bufs=1))
        sbuf = ctx.enter_context(tc.tile_pool(name="sbuf", bufs=1))
        psum = ctx.enter_context(tc.psum_pool(name="psum", bufs=8))

        def tile(shape, dtype, name, after=None):
            return sbuf.tile(shape, dtype, name=name, tag=after or name, align_bytes=64)

        def quantize(values, name):
            width = values.shape[1] // PACK
            codes = tile([P, width], U32, f"{name}_codes")
            scales = tile([P, width], U8, f"{name}_scales")
            nc.vector.quantize_mx(out=codes[:].bitcast(FP8X4), scales=scales[:], in_=values)
            return codes, scales

        def woven(flat):
            return flat.rearrange("p (c i t) -> p c t i", i=4, t=PACK)

        def planes(stacked):
            return stacked.rearrange("p t (c i) -> p c t i", i=4)

        offs_t = lists.tile([P, S // LIST_ROWS], U16, name="offs_t")
        n1_t = lists.tile([P, S // LIST_ROWS], U16, name="n1_t")
        n2_t = lists.tile([P, V // LIST_ROWS], U16, name="n2_t")
        xs_all = tile([P, T], U8, "xs_all")
        xw_all = tile([P, T], U32, "xw_all")
        w1_raw = tile([P, PACK, H], F32, "w1_raw")
        nc.vector.memset(xs_all[:].bitcast(I32), 0)
        nc.sync.dma_start(offs_t[:], offs)
        nc.sync.dma_start(out=xw_all[:, :X_FIRST].bitcast(I32), in_=words_i32(x_words)[:, :X_FIRST])
        for q in range(QUADRANTS):
            in_sbuf, in_hbm = scale_rows(xs_all, x_scales, q)
            nc.sync.dma_start(out=in_sbuf, in_=in_hbm)
        nc.sync.dma_start(out=xw_all[:, X_FIRST:].bitcast(I32), in_=words_i32(x_words)[:, X_FIRST:])
        nc.sync.dma_start(out=w1_raw[:], in_=w1.rearrange("(p j) c -> p j c", j=PACK))
        nc.sync.dma_start(n1_t[:], n1)
        nc.sync.dma_start(n2_t[:], n2)

        xs = tile([P, S], U8, "xs")
        nc.vector.tensor_copy(xs[:], xs_all[:].indirect(offs_t[:]))
        xw = [tile([P, BANK], U32, f"xw{half}") for half in range(S // BANK)]
        for half in range(S // BANK):
            nc.vector.tensor_copy(xw[half][:], xw_all[:].indirect(entries(offs_t, half * BANK, BANK)))

        w1_view = w1_raw[:].rearrange("p j (b t h i) -> p t b h j i", t=PACK, h=2, i=4)
        w1_mx = []
        for t in range(PACK):
            w1_bf = tile([P, P * PACK], BF16, f"w1_bf{t}")
            nc.scalar.copy(w1_bf[:].rearrange("p (b h i j) -> p b h j i", h=2, i=4, j=PACK), w1_view[:, t])
            w1_mx.append(quantize(w1_bf[:], f"w1_{t}"))

        w2_raw = tile([P, PACK, H], F32, "w2_raw", after="xw_all")
        w2_rows = w2.rearrange("(b j i) c -> j b i c", j=PACK, i=8)
        for j in range(PACK):
            nc.sync.dma_start(out=w2_raw[:, j, :], in_=w2_rows[j])
        w3w_raw = tile([P, N], U32, "w3w_raw", after="w1_raw")
        nc.sync.dma_start(out=w3w_raw[:].bitcast(I32), in_=words_i32(w3_words))
        w3s_raw = tile([P, N], U8, "w3s_raw", after="xs_all")
        nc.vector.memset(w3s_raw[:].bitcast(I32), 0)
        for q in range(QUADRANTS):
            in_sbuf, in_hbm = scale_rows(w3s_raw, w3_scales, q)
            nc.sync.dma_start(out=in_sbuf, in_=in_hbm)

        y = []
        for t in range(PACK):
            y_t = tile([P, S], F32, f"y{t}")
            codes, scales = w1_mx[t]
            width = BANK // 2 if t == 0 else BANK
            for first in range(0, S, width):
                cols = slice(first, first + width)
                acc = psum.tile([P, width], F32, name="bank")
                product(acc[:], codes[:], scales[:], xw[first // BANK][:, first % BANK : first % BANK + width], xs[:, cols])
                if t == 0 and first + width < S:
                    nc.vector.tensor_copy(y_t[:, cols], acc[:])
                else:
                    nc.scalar.copy(y_t[:, cols], acc[:])
            y.append(y_t)

        w2_bf = tile([P, H * PACK], BF16, "w2_bf", after="xw1")
        w2_dst = w2_bf[:].rearrange("p (t m j) -> p m j t", t=PACK, j=PACK)
        w2_src = w2_raw[:].rearrange("p j (m t) -> p m j t", t=PACK)
        for half in range(2):
            nc.scalar.copy(w2_dst[:, 64 * half : 64 * half + 64], w2_src[:, 64 * half : 64 * half + 64])
        res_t = tile([P, PACK, V], F32, "res_t", after="xw0")
        nc.sync.dma_start(out=res_t[:], in_=res.rearrange("(p t) v -> p t v", t=PACK))

        def line_up(first, count, dtype, after=None):
            lined = tile([P, PACK, 2 * count], dtype, f"lined{first}", after)
            for t in range(PACK):
                nc.vector.tensor_copy(lined[:, t, :], y[t][:].indirect(entries(n1_t, 2 * first, 2 * count)))
            return lined

        lined_a = line_up(0, PIECE, F32)
        lined_b = line_up(PIECE, 2 * PIECE, F32)
        sides = []
        for c, lined in enumerate([lined_a[:], lined_b[:, :, : 2 * PIECE], lined_b[:, :, 2 * PIECE :]]):
            both = tile([P, 2, PACK * PIECE], BF16, f"sides{c}")
            nc.scalar.copy(
                both[:].rearrange("p e (c i t) -> p c t i e", i=2, t=PACK),
                lined.rearrange("p t (c i e) -> p c t i e", i=2, e=2),
            )
            sides.append(both)
        w2_codes, w2_scales = quantize(w2_bf[:], "w2")

        h = [tile([P, V], F32, f"h{t}") for t in range(PACK)]
        h_acc = [psum.tile([P, V], F32, name="bank") for t in range(PACK)]

        def hidden(z_bf, first):
            z_codes, z_scales = quantize(z_bf[:], f"z{first}")
            cols = slice(first, first + z_codes.shape[1])
            for t in range(PACK):
                rows = slice(t * P, (t + 1) * P)
                product(h_acc[t][:, cols], w2_codes[:, rows], w2_scales[:, rows], z_codes[:], z_scales[:])
                nc.scalar.copy(h[t][:, cols], h_acc[t][:, cols])

        for c in range(2):
            z_bf = tile([P, PACK * PIECE], BF16, f"z_bf{c}")
            nc.vector.tensor_tensor(z_bf[:], sides[c][:, 0, :], sides[c][:, 1, :], MAX)
            hidden(z_bf, c * PIECE)
        lined_c = line_up(3 * PIECE, PIECE, BF16, after="sides0")
        z_rest = tile([P, 2 * PACK * PIECE], BF16, "z_rest")
        nc.vector.tensor_tensor(z_rest[:, : PACK * PIECE], sides[2][:, 0, :], sides[2][:, 1, :], MAX)
        pairs = lined_c[:].rearrange("p t (c i e) -> p e c t i", i=4, e=2)
        nc.vector.tensor_tensor(woven(z_rest[:, PACK * PIECE :]), pairs[:, 0], pairs[:, 1], MAX)
        hidden(z_rest, 2 * PIECE)

        w3_codes = tile([P, N], U32, "w3_codes", after="z_rest")
        nc.vector.tensor_copy(
            w3_codes[:].rearrange("p (t c i) -> p c t i", t=PACK, i=4),
            w3w_raw[:].rearrange("p (c i t) -> p c t i", t=PACK, i=4),
        )
        w3_bytes = tile([P, N], U8, "w3_bytes", after="sides0")
        nc.vector.tensor_copy(
            w3_bytes[:].rearrange("p (t m) -> p t m", t=PACK), w3s_raw[:].rearrange("p (m t) -> p t m", t=PACK)
        )

        h_bf = tile([P, PACK, V], BF16, "h_bf")
        for t in range(PACK):
            nc.scalar.copy(h_bf[:, t, :], h_acc[t][:])
        z2_bf = [tile([P, PACK * PIECE], BF16, f"z2_bf{c}") for c in range(PIECES)]

        def fetch_partners(first, count, after=None):
            partner = tile([P, PACK, count], BF16, f"partner{first}", after)
            for t in range(PACK):
                nc.vector.tensor_copy(partner[:, t, :], h[t][:].indirect(entries(n2_t, first, count)))
            return partner[:], h_bf[:, :, first : first + count]

        for first, count in ((0, PIECE), (PIECE, 2 * PIECE)):
            partner, own = fetch_partners(first, count)
            larger = tile([P, PACK, count], BF16, f"larger{first}")
            nc.vector.tensor_tensor(larger[:], partner, own, MAX)
            for offset in range(0, count, PIECE):
                nc.scalar.copy(woven(z2_bf[(first + offset) // PIECE][:]), planes(larger[:, :, offset : offset + PIECE]))

        out_rows = out_0.rearrange("(p t) v -> p t v", t=PACK)
        out_scales = tile([P, V], U8, "out_scales")

        def finish(c, round_on):
            cols = slice(c * PIECE, (c + 1) * PIECE)
            z2_codes, z2_scales = quantize(z2_bf[c][:], f"z2_{c}")
            acc = psum.tile([P, PACK, PIECE], F32, name="bank")
            for t in range(PACK):
                rows = slice(t * P, (t + 1) * P)
                product(acc[:, t, :], w3_codes[:, rows], w3_bytes[:, rows], z2_codes[:], z2_scales[:])
            total = tile([P, PACK, PIECE], F32, f"total{c}")
            nc.vector.tensor_tensor(total[:], acc[:], res_t[:, :, cols], ADD)
            nc.sync.dma_start(out=out_rows[:, :, cols], in_=total[:])
            total_bf = tile([P, PACK * PIECE], BF16, f"total_bf{c}")
            round_on(woven(total_bf[:]), planes(total[:]))
            out_codes = tile([P, PIECE], U32, f"out_codes{c}")
            nc.vector.quantize_mx(out=out_codes[:].bitcast(FP8X4), scales=out_scales[:, cols], in_=total_bf[:])
            nc.sync.dma_start(out=words_i32(out_1)[:, cols], in_=out_codes[:].bitcast(I32))

        finish(0, nc.scalar.copy)
        partner, own = fetch_partners(3 * PIECE, PIECE, after="partner0")
        nc.vector.tensor_tensor(woven(z2_bf[3][:]), planes(partner), planes(own), MAX)
        finish(1, nc.scalar.copy)
        finish(3, nc.scalar.copy)
        finish(2, nc.vector.tensor_copy)
        for q in range(QUADRANTS):
            in_sbuf, in_hbm = scale_rows(out_scales, out_2, q)
            queue = nc.scalar if q % 2 == 0 else nc.sync
            queue.dma_start(out=in_hbm, in_=in_sbuf)
